import numpy as np
import ml_dtypes


def mxq(x, axis, fmt="e4m3"):
    dtype, down = {"e4m3": (ml_dtypes.float8_e4m3fn, 7), "e5m2": (ml_dtypes.float8_e5m2, 14)}[fmt]
    v = np.moveaxis(np.asarray(x, np.float32).astype(ml_dtypes.bfloat16).astype(np.float64), axis, -1)
    blocks = v.reshape(v.shape[:-1] + (-1, 32))
    amax = np.abs(blocks).max(-1, keepdims=True)
    byte = np.maximum(np.where(amax > 0, np.frexp(amax)[1] - 1 + 127, 0) - down, 1)
    scale = np.exp2(byte - 127.0)
    codes = (blocks / scale).astype(np.float32).astype(dtype).astype(np.float64)
    return np.moveaxis((codes * scale).reshape(v.shape), -1, axis)


WIDE = False


def mx_kscale(k):
    if not WIDE:
        return np.ones(k)
    levels = np.array([10, -10, 5, -5, 0])
    if k % 512:
        return np.exp2(np.random.permutation(np.resize(levels, k // 32))).repeat(32)
    a = np.empty((k // 512, 16))
    for p in range(k // 512):
        a[p, :8] = np.random.permutation(np.resize(levels, 8))
        for g in range(8):
            far = levels[np.abs(levels - a[p, g]) >= 10]
            a[p, g + 8] = far[np.random.randint(len(far))]
    return np.exp2(a.ravel()).repeat(32)


def f64(x):
    return np.asarray(x).astype(np.float64)


def striped(idx):
    return np.tile(idx.reshape(-1, 16).T, (8, 1)).astype(np.uint16)


def unstriped(offs):
    return offs[:16].T.reshape(-1).astype(np.int64)


K, T, S, H, N = 1024, 1024, 512, 512, 256
P = 2 ** 7


def setup_inputs():
    n = np.random.standard_normal
    s = mx_kscale(K)[:, None]
    u = mx_kscale(H)
    return {
        "xT": (n((K, T)) * s).astype(np.float32),
        "w1": (n((K, H)) / np.sqrt(K) / s * u).astype(np.float32),
        "w2": (n((H, N)) / np.sqrt(H) / u[:, None]).astype(np.float32),
        "lam": np.tile(np.random.uniform(0.1, 0.9, S), (P, 1)).astype(np.float32),
        "mu": np.tile(np.random.uniform(0.1, 0.9, S), (P, 1)).astype(np.float32),
        "offs": striped(np.random.permutation(T)[:S]),
        "pos1": striped(np.random.permutation(S)),
    }


def reference(xT, w1, w2, lam, mu, offs, pos1):
    xq = mxq(f64(xT)[:, unstriped(offs)], 0, "e4m3")
    h = mxq(f64(w1), 0, "e4m3").T @ xq
    z = h * f64(lam)[:1] + h[:, unstriped(pos1)] * f64(mu)[:1]
    return mxq(f64(w2), 0, "e4m3").T @ mxq(z, 0, "e4m3")

@@ -1,0 +1,179 @@
+from contextlib import ExitStack
+
+import concourse.mybir as mybir
+
+K, T, S, H, N = 1024, 1024, 512, 512, 256
+FLOPS = 2 * K * H * S + 2 * H * N * S
+
+F32 = mybir.dt.float32
+BF16 = mybir.dt.bfloat16
+I32 = mybir.dt.int32
+U32 = mybir.dt.uint32
+U16 = mybir.dt.uint16
+U8 = mybir.dt.uint8
+FP8X4 = mybir.dt.float8_e4m3fn_x4
+MULT = mybir.AluOpType.mult
+ADD = mybir.AluOpType.add
+
+P = 128
+PACK = 4
+K_PASS = P * PACK
+PASSES = K // K_PASS
+LINE = 4
+LIST_ROWS = 16
+HALF = S // 2
+X_SCALAR = (640, 640, 640, 512)
+W1_SCALAR = (80, 44)
+OUT_CHUNKS = ((0, 256), (256, 384), (384, 512))
+
+
+def tile_picked_mixup_none_e_kernel(tc, xT, w1, w2, lam, mu, offs, pos1, out):
+    nc = tc.nc
+
+    with ExitStack() as ctx:
+        sb = ctx.enter_context(tc.tile_pool(name="sb", bufs=1))
+        psum = ctx.enter_context(tc.psum_pool(name="psum", bufs=1))
+
+        def tile(name, shape, dtype):
+            return sb.tile(shape, dtype, name=name, align_bytes=64)
+
+        offs_sb = sb.tile([P, S // LIST_ROWS], U16, name="offs_sb")
+        pos_sb = sb.tile([P, S // LIST_ROWS], U16, name="pos_sb")
+        x_raw = [tile("x_raw%d" % i, [P, 2, T], F32) for i in range(2 * PASSES)]
+        w1_raw = [tile("w1_raw%d" % g, [P, PACK, H], F32) for g in range(PASSES)]
+        w2_raw = tile("w2_raw", [P, PACK, N], F32)
+        mu_sb = tile("mu_sb", [P, S], F32)
+        lam_sb = tile("lam_sb", [P, S], F32)
+        x_view = xT.rearrange("(g p u e) t -> g u p e t", p=P, u=2, e=2)
+        for i in range(2 * PASSES):
+            nc.sync.dma_start(out=x_raw[i][:], in_=x_view[i // 2, i % 2])
+            if i == 0:
+                nc.sync.dma_start(offs_sb[:], offs)
+        w1_view = w1.rearrange("(g p j) c -> g p j c", p=P, j=PACK)
+        for g in range(PASSES):
+            nc.sync.dma_start(out=w1_raw[g][:], in_=w1_view[g])
+        nc.sync.dma_start(out=w2_raw[:], in_=w2.rearrange("(p j) c -> p j c", j=PACK))
+        nc.sync.dma_start(pos_sb[:], pos1)
+        nc.sync.dma_start(out=mu_sb[:], in_=mu)
+        nc.sync.dma_start(out=lam_sb[:], in_=lam)
+
+        x_codes = [tile("x_codes%d" % g, [P, S], U32) for g in range(PASSES)]
+        x_scales = [tile("x_scales%d" % g, [P, S], U8) for g in range(PASSES)]
+        for g in range(PASSES):
+            picked = tile("picked%d" % g, [P, 2, 2 * S], BF16)
+            for u in range(2):
+                i = 2 * g + u
+                pairs = tile("pairs%d" % i, [P, T, 2], BF16)
+                cut = X_SCALAR[i]
+                for copy, cols in ((nc.scalar.copy, slice(0, cut)), (nc.vector.tensor_copy, slice(cut, T))):
+                    copy(
+                        out=pairs[:, cols, :].rearrange("p (c i) e -> p c e i", i=LINE),
+                        in_=x_raw[i][:, :, cols].rearrange("p e (c i) -> p c e i", i=LINE),
+                    )
+                window = pairs[:].rearrange("p t e -> p (t e)").bitcast(U32)
+                nc.vector.tensor_copy(out=picked[:, u, :].bitcast(U32), in_=window.indirect(offs_sb[:]))
+            woven = tile("woven%d" % g, [P, S * PACK], BF16)
+            copy, word = (nc.scalar.copy, U32) if g == 0 else (nc.vector.tensor_copy, I32)
+            copy(
+                out=woven[:].bitcast(word).rearrange("p (c i u) -> p c u i", i=LINE, u=2),
+                in_=picked[:].rearrange("p u n -> p (u n)").bitcast(word).rearrange("p (u c i) -> p c u i", u=2, i=LINE),
+            )
+            nc.vector.quantize_mx(out=x_codes[g][:].bitcast(FP8X4), scales=x_scales[g][:], in_=woven[:])
+
+        h_ps = [psum.tile([P, S], F32, name="h_ps%d" % t) for t in range(PACK)]
+        for g in range(PASSES):
+            grouped = tile("w1_grouped%d" % g, [P, PACK, P, PACK], BF16)
+            cut = W1_SCALAR[g]
+            for copy, ms in ((nc.scalar.copy, slice(0, cut)), (nc.vector.tensor_copy, slice(cut, P))):
+                copy(
+                    out=grouped[:, :, ms, :].rearrange("p t m j -> p m j t"),
+                    in_=w1_raw[g][:].rearrange("p j (m t) -> p m j t", t=PACK)[:, ms],
+                )
+            for t in range(PACK):
+                codes = tile("w1_codes%d_%d" % (g, t), [P, P], U32)
+                scales = tile("w1_scales%d_%d" % (g, t), [P, P], U8)
+                nc.vector.quantize_mx(
+                    out=codes[:].bitcast(FP8X4), scales=scales[:], in_=grouped[:, t].rearrange("p m j -> p (m j)")
+                )
+                nc.tensor.matmul_mx(
+                    out=h_ps[t][:],
+                    lhsT=codes[:].bitcast(FP8X4),
+                    lhsT_scale=scales[:],
+                    rhs=x_codes[g][:].bitcast(FP8X4),
+                    rhs_scale=x_scales[g][:],
+                    start=(g == 0),
+                    stop=(g == PASSES - 1),
+                )
+
+        w2_grouped = tile("w2_grouped", [P, N, PACK], BF16)
+        nc.vector.tensor_copy(
+            out=w2_grouped[:].rearrange("p (c i) j -> p c j i", i=LINE),
+            in_=w2_raw[:].rearrange("p j (c i) -> p c j i", i=LINE),
+        )
+        w2_codes = tile("w2_codes", [P, N], U32)
+        w2_scales = tile("w2_scales", [P, N], U8)
+
+        h_sb = [tile("h_sb%d" % t, [P, S], F32) for t in range(PACK)]
+        own = tile("own", [P, PACK, S], F32)
+        partner = tile("partner", [P, PACK, S], F32)
+
+        def fetch(t, half):
+            cols = slice(half * HALF, (half + 1) * HALF)
+            places = pos_sb[:, half * HALF // LIST_ROWS : (half + 1) * HALF // LIST_ROWS]
+            nc.vector.tensor_tensor(partner[:, t, cols], h_sb[t][:].indirect(places), mu_sb[:, cols], MULT)
+
+        z_bf = [tile("z_bf%d" % c, [P, hi - lo, PACK], BF16) for c, (lo, hi) in enumerate(OUT_CHUNKS)]
+
+        def mix(c):
+            lo, hi = OUT_CHUNKS[c]
+            nc.vector.tensor_tensor(
+                z_bf[c][:].rearrange("p (c i) t -> p c t i", i=LINE),
+                own[:, :, lo:hi].rearrange("p t (c i) -> p c t i", i=LINE),
+                partner[:, :, lo:hi].rearrange("p t (c i) -> p c t i", i=LINE),
+                ADD,
+            )
+
+        out_view = out.rearrange("(b p) s -> p b s", p=P)
+
+        def finish(c):
+            lo, hi = OUT_CHUNKS[c]
+            width = hi - lo
+            z_codes = tile("z_codes%d" % c, [P, width], U32)
+            z_scales = tile("z_scales%d" % c, [P, width], U8)
+            nc.vector.quantize_mx(
+                out=z_codes[:].bitcast(FP8X4), scales=z_scales[:], in_=z_bf[c][:].rearrange("p n t -> p (n t)")
+            )
+            o_ps = psum.tile([P, N // P, width], F32, name="o_ps%d" % c)
+            for b in range(N // P):
+                nc.tensor.matmul_mx(
+                    out=o_ps[:, b, :],
+                    lhsT=w2_codes[:, b * P : (b + 1) * P].bitcast(FP8X4),
+                    lhsT_scale=w2_scales[:, b * P : (b + 1) * P],
+                    rhs=z_codes[:].bitcast(FP8X4),
+                    rhs_scale=z_scales[:],
+                    start=True,
+                    stop=True,
+                )
+            o_sb = tile("o_sb%d" % c, [P, N // P, width], F32)
+            nc.scalar.copy(out=o_sb[:], in_=o_ps[:])
+            nc.sync.dma_start(out=out_view[:, :, lo:hi], in_=o_sb[:])
+
+        for t in range(PACK):
+            nc.scalar.copy(out=h_sb[t][:], in_=h_ps[t][:])
+            fetch(t, 0)
+            if t == 0:
+                nc.vector.quantize_mx(
+                    out=w2_codes[:].bitcast(FP8X4),
+                    scales=w2_scales[:],
+                    in_=w2_grouped[:].rearrange("p n j -> p (n j)"),
+                )
+            nc.vector.tensor_tensor(own[:, t, :], h_sb[t][:], lam_sb[:], MULT)
+        mix(0)
+        fetch(0, 1)
+        finish(0)
+        for t in range(1, PACK):
+            fetch(t, 1)
+        mix(1)
+        mix(2)
+        finish(1)
+        finish(2)

@@ -1,6 +1,7 @@
 from contextlib import ExitStack
 
 import concourse.mybir as mybir
+from concourse.masks import make_identity
 
 K, T, S, H, N = 1024, 1024, 512, 512, 256
 FLOPS = 2 * K * H * S + 2 * H * N * S
@@ -14,6 +15,7 @@ U8 = mybir.dt.uint8
 FP8X4 = mybir.dt.float8_e4m3fn_x4
 MULT = mybir.AluOpType.mult
 ADD = mybir.AluOpType.add
+COPY = mybir.ActivationFunctionType.Copy
 
 P = 128
 PACK = 4
@@ -21,10 +23,10 @@ K_PASS = P * PACK
 PASSES = K // K_PASS
 LINE = 4
 LIST_ROWS = 16
-HALF = S // 2
-X_SCALAR = (640, 640, 640, 512)
-W1_SCALAR = (80, 44)
-OUT_CHUNKS = ((0, 256), (256, 384), (384, 512))
+SPARE = 16
+BLOCKS = S // P
+X_SCALAR = 352
+W1_SCALAR = (104, 64)
 
 
 def tile_picked_mixup_none_e_kernel(tc, xT, w1, w2, lam, mu, offs, pos1, out):
@@ -34,8 +36,25 @@ def tile_picked_mixup_none_e_kernel(tc, xT, w1, w2, lam, mu, offs, pos1, out):
         sb = ctx.enter_context(tc.tile_pool(name="sb", bufs=1))
         psum = ctx.enter_context(tc.psum_pool(name="psum", bufs=1))
 
-        def tile(name, shape, dtype):
-            return sb.tile(shape, dtype, name=name, align_bytes=64)
+        def tile(name, shape, dtype, tag=None):
+            return sb.tile(shape, dtype, name=name, tag=tag or name, align_bytes=64)
+
+        def quantize(name, values, width, tag=None):
+            codes = tile(name + "_codes", [P, width], U32, tag=tag)
+            scales = tile(name + "_scales", [P, width], U8)
+            nc.vector.quantize_mx(out=codes[:].bitcast(FP8X4), scales=scales[:], in_=values)
+            return codes, scales
+
+        def product(acc, left, cols, right, start, stop):
+            nc.tensor.matmul_mx(
+                out=acc,
+                lhsT=left[0][:, cols].bitcast(FP8X4),
+                lhsT_scale=left[1][:, cols],
+                rhs=right[0][:].bitcast(FP8X4),
+                rhs_scale=right[1][:],
+                start=start,
+                stop=stop,
+            )
 
         offs_sb = sb.tile([P, S // LIST_ROWS], U16, name="offs_sb")
         pos_sb = sb.tile([P, S // LIST_ROWS], U16, name="pos_sb")
@@ -43,7 +62,7 @@ def tile_picked_mixup_none_e_kernel(tc, xT, w1, w2, lam, mu, offs, pos1, out):
         w1_raw = [tile("w1_raw%d" % g, [P, PACK, H], F32) for g in range(PASSES)]
         w2_raw = tile("w2_raw", [P, PACK, N], F32)
         mu_sb = tile("mu_sb", [P, S], F32)
-        lam_sb = tile("lam_sb", [P, S], F32)
+        lam_col = tile("lam_col", [P, BLOCKS], F32)
         x_view = xT.rearrange("(g p u e) t -> g u p e t", p=P, u=2, e=2)
         for i in range(2 * PASSES):
             nc.sync.dma_start(out=x_raw[i][:], in_=x_view[i // 2, i % 2])
@@ -55,125 +74,115 @@ def tile_picked_mixup_none_e_kernel(tc, xT, w1, w2, lam, mu, offs, pos1, out):
         nc.sync.dma_start(out=w2_raw[:], in_=w2.rearrange("(p j) c -> p j c", j=PACK))
         nc.sync.dma_start(pos_sb[:], pos1)
         nc.sync.dma_start(out=mu_sb[:], in_=mu)
-        nc.sync.dma_start(out=lam_sb[:], in_=lam)
+        with nc.allow_non_contiguous_dma(reason="one share a partition"):
+            nc.sync.dma_start(out=lam_col[:], in_=lam[0:1, :].rearrange("o (b p) -> p (o b)", p=P))
 
-        x_codes = [tile("x_codes%d" % g, [P, S], U32) for g in range(PASSES)]
-        x_scales = [tile("x_scales%d" % g, [P, S], U8) for g in range(PASSES)]
-        for g in range(PASSES):
-            picked = tile("picked%d" % g, [P, 2, 2 * S], BF16)
-            for u in range(2):
-                i = 2 * g + u
-                pairs = tile("pairs%d" % i, [P, T, 2], BF16)
-                cut = X_SCALAR[i]
-                for copy, cols in ((nc.scalar.copy, slice(0, cut)), (nc.vector.tensor_copy, slice(cut, T))):
-                    copy(
-                        out=pairs[:, cols, :].rearrange("p (c i) e -> p c e i", i=LINE),
-                        in_=x_raw[i][:, :, cols].rearrange("p e (c i) -> p c e i", i=LINE),
-                    )
-                window = pairs[:].rearrange("p t e -> p (t e)").bitcast(U32)
-                nc.vector.tensor_copy(out=picked[:, u, :].bitcast(U32), in_=window.indirect(offs_sb[:]))
-            woven = tile("woven%d" % g, [P, S * PACK], BF16)
-            copy, word = (nc.scalar.copy, U32) if g == 0 else (nc.vector.tensor_copy, I32)
+        ident = tile("ident", [P, P], F32)
+        make_identity(nc, ident[:])
+        h_sb = [tile("h_sb%d" % t, [P, S + SPARE], F32) for t in range(PACK)]
+        for t in range(PACK):
+            nc.gpsimd.memset(h_sb[t][:, S:], 0.0)
+
+        picked = [tile("picked%d" % g, [P, 2, 2 * S], BF16) for g in range(PASSES)]
+
+        def pick(i):
+            pairs = tile("pairs%d" % i, [P, T, 2], BF16)
+            for copy, cols in ((nc.scalar.copy, slice(0, X_SCALAR)), (nc.vector.tensor_copy, slice(X_SCALAR, T))):
+                copy(
+                    out=pairs[:, cols, :].rearrange("p (c i) e -> p c e i", i=LINE),
+                    in_=x_raw[i][:, :, cols].rearrange("p e (c i) -> p c e i", i=LINE),
+                )
+            window = pairs[:].rearrange("p t e -> p (t e)").bitcast(U32)
+            nc.vector.tensor_copy(out=picked[i // 2][:, i % 2, :].bitcast(U32), in_=window.indirect(offs_sb[:]))
+
+        def weave(g, copy, word, tag):
+            woven = tile("woven%d" % g, [P, S * PACK], BF16, tag=tag)
+            words = picked[g][:].rearrange("p u n -> p (u n)").bitcast(word)
             copy(
                 out=woven[:].bitcast(word).rearrange("p (c i u) -> p c u i", i=LINE, u=2),
-                in_=picked[:].rearrange("p u n -> p (u n)").bitcast(word).rearrange("p (u c i) -> p c u i", u=2, i=LINE),
+                in_=words.rearrange("p (u c i) -> p c u i", u=2, i=LINE),
             )
-            nc.vector.quantize_mx(out=x_codes[g][:].bitcast(FP8X4), scales=x_scales[g][:], in_=woven[:])
+            return quantize("x%d" % g, woven[:], S)
 
-        h_ps = [psum.tile([P, S], F32, name="h_ps%d" % t) for t in range(PACK)]
-        for g in range(PASSES):
-            grouped = tile("w1_grouped%d" % g, [P, PACK, P, PACK], BF16)
+        for i in range(2 * PASSES):
+            pick(i)
+        xq = [weave(0, nc.scalar.copy, U32, "x_raw3"), weave(1, nc.vector.tensor_copy, I32, None)]
+
+        grouped = [tile("w1_grouped%d" % g, [P, PACK, P, PACK], BF16) for g in range(PASSES)]
+
+        def group(g):
             cut = W1_SCALAR[g]
             for copy, ms in ((nc.scalar.copy, slice(0, cut)), (nc.vector.tensor_copy, slice(cut, P))):
                 copy(
-                    out=grouped[:, :, ms, :].rearrange("p t m j -> p m j t"),
+                    out=grouped[g][:, :, ms, :].rearrange("p t m j -> p m j t"),
                     in_=w1_raw[g][:].rearrange("p j (m t) -> p m j t", t=PACK)[:, ms],
                 )
-            for t in range(PACK):
-                codes = tile("w1_codes%d_%d" % (g, t), [P, P], U32)
-                scales = tile("w1_scales%d_%d" % (g, t), [P, P], U8)
-                nc.vector.quantize_mx(
-                    out=codes[:].bitcast(FP8X4), scales=scales[:], in_=grouped[:, t].rearrange("p m j -> p (m j)")
-                )
-                nc.tensor.matmul_mx(
-                    out=h_ps[t][:],
-                    lhsT=codes[:].bitcast(FP8X4),
-                    lhsT_scale=scales[:],
-                    rhs=x_codes[g][:].bitcast(FP8X4),
-                    rhs_scale=x_scales[g][:],
-                    start=(g == 0),
-                    stop=(g == PASSES - 1),
-                )
+
+        w1q = {}
+
+        def quantize_w1(g, first, count, tag=None):
+            values = grouped[g][:, first : first + count].rearrange("p t m j -> p (t m j)")
+            planes = quantize("w1_%d_%d" % (g, first), values, count * P, tag=tag)
+            for n in range(count):
+                w1q[g, first + n] = (planes, slice(n * P, (n + 1) * P))
+
+        group(0)
+        quantize_w1(0, 0, 2)
+        group(1)
+        quantize_w1(1, 0, 1)
+        quantize_w1(1, 1, 1)
+        quantize_w1(0, 2, 2, tag="w1_raw1")
+        quantize_w1(1, 2, 2)
+        h_ps = [psum.tile([P, S], F32, name="h_ps%d" % t, tag="bank_a%d" % t) for t in range(PACK)]
+        for t in range(PACK):
+            for g in range(PASSES):
+                product(h_ps[t][:], w1q[g, t][0], w1q[g, t][1], xq[g], g == 0, g == PASSES - 1)
 
         w2_grouped = tile("w2_grouped", [P, N, PACK], BF16)
-        nc.vector.tensor_copy(
+        nc.scalar.copy(
             out=w2_grouped[:].rearrange("p (c i) j -> p c j i", i=LINE),
             in_=w2_raw[:].rearrange("p j (c i) -> p c j i", i=LINE),
         )
-        w2_codes = tile("w2_codes", [P, N], U32)
-        w2_scales = tile("w2_scales", [P, N], U8)
+        w2q = quantize("w2", w2_grouped[:].rearrange("p n j -> p (n j)"), N)
 
-        h_sb = [tile("h_sb%d" % t, [P, S], F32) for t in range(PACK)]
-        own = tile("own", [P, PACK, S], F32)
         partner = tile("partner", [P, PACK, S], F32)
+        turned_ps = [psum.tile([P, PACK, P], F32, name="turned_ps%d" % b, tag="bank_b%d" % b) for b in range(BLOCKS)]
+        for t in range(PACK):
+            nc.scalar.copy(out=h_sb[t][:, :S], in_=h_ps[t][:])
+            nc.vector.tensor_tensor(partner[:, t, :], h_sb[t][:].indirect(pos_sb[:]), mu_sb[:], MULT)
+            for b in range(BLOCKS):
+                nc.tensor.transpose(turned_ps[b][:, t, :], h_sb[t][:, b * P : (b + 1) * P], ident[:])
 
-        def fetch(t, half):
-            cols = slice(half * HALF, (half + 1) * HALF)
-            places = pos_sb[:, half * HALF // LIST_ROWS : (half + 1) * HALF // LIST_ROWS]
-            nc.vector.tensor_tensor(partner[:, t, cols], h_sb[t][:].indirect(places), mu_sb[:, cols], MULT)
+        own_ps = []
+        for b in range(BLOCKS):
+            turned = tile("turned%d" % b, [P, PACK, P], F32)
+            nc.scalar.activation(turned[:], turned_ps[b][:], COPY, scale=lam_col[:, b : b + 1])
+            own_ps.append(psum.tile([P, PACK, P], F32, name="own_ps%d" % b, tag="bank_a%d" % b))
+            for t in range(PACK):
+                nc.tensor.transpose(own_ps[b][:, t, :], turned[:, t, :], ident[:])
 
-        z_bf = [tile("z_bf%d" % c, [P, hi - lo, PACK], BF16) for c, (lo, hi) in enumerate(OUT_CHUNKS)]
+        z_bf = [tile("z_bf%d" % b, [P, P, PACK], BF16) for b in range(BLOCKS)]
+        out_view = out.rearrange("(r p) s -> p r s", p=P)
 
-        def mix(c):
-            lo, hi = OUT_CHUNKS[c]
+        def mix(b):
             nc.vector.tensor_tensor(
-                z_bf[c][:].rearrange("p (c i) t -> p c t i", i=LINE),
-                own[:, :, lo:hi].rearrange("p t (c i) -> p c t i", i=LINE),
-                partner[:, :, lo:hi].rearrange("p t (c i) -> p c t i", i=LINE),
+                z_bf[b][:].rearrange("p (c i) t -> p c t i", i=LINE),
+                own_ps[b][:].rearrange("p t (c i) -> p c t i", i=LINE),
+                partner[:, :, b * P : (b + 1) * P].rearrange("p t (c i) -> p c t i", i=LINE),
                 ADD,
             )
 
-        out_view = out.rearrange("(b p) s -> p b s", p=P)
-
-        def finish(c):
-            lo, hi = OUT_CHUNKS[c]
-            width = hi - lo
-            z_codes = tile("z_codes%d" % c, [P, width], U32)
-            z_scales = tile("z_scales%d" % c, [P, width], U8)
-            nc.vector.quantize_mx(
-                out=z_codes[:].bitcast(FP8X4), scales=z_scales[:], in_=z_bf[c][:].rearrange("p n t -> p (n t)")
-            )
-            o_ps = psum.tile([P, N // P, width], F32, name="o_ps%d" % c)
-            for b in range(N // P):
-                nc.tensor.matmul_mx(
-                    out=o_ps[:, b, :],
-                    lhsT=w2_codes[:, b * P : (b + 1) * P].bitcast(FP8X4),
-                    lhsT_scale=w2_scales[:, b * P : (b + 1) * P],
-                    rhs=z_codes[:].bitcast(FP8X4),
-                    rhs_scale=z_scales[:],
-                    start=True,
-                    stop=True,
-                )
-            o_sb = tile("o_sb%d" % c, [P, N // P, width], F32)
+        def finish(b):
+            zq = quantize("z%d" % b, z_bf[b][:].rearrange("p n t -> p (n t)"), P)
+            o_ps = psum.tile([P, N // P, P], F32, name="o_ps%d" % b, tag="bank_b%d" % b)
+            for r in range(N // P):
+                product(o_ps[:, r, :], w2q, slice(r * P, (r + 1) * P), zq, True, True)
+            o_sb = tile("o_sb%d" % b, [P, N // P, P], F32)
             nc.scalar.copy(out=o_sb[:], in_=o_ps[:])
-            nc.sync.dma_start(out=out_view[:, :, lo:hi], in_=o_sb[:])
+            nc.sync.dma_start(out=out_view[:, :, b * P : (b + 1) * P], in_=o_sb[:])
 
-        for t in range(PACK):
-            nc.scalar.copy(out=h_sb[t][:], in_=h_ps[t][:])
-            fetch(t, 0)
-            if t == 0:
-                nc.vector.quantize_mx(
-                    out=w2_codes[:].bitcast(FP8X4),
-                    scales=w2_scales[:],
-                    in_=w2_grouped[:].rearrange("p n j -> p (n j)"),
-                )
-            nc.vector.tensor_tensor(own[:, t, :], h_sb[t][:], lam_sb[:], MULT)
         mix(0)
-        fetch(0, 1)
-        finish(0)
-        for t in range(1, PACK):
-            fetch(t, 1)
-        mix(1)
-        mix(2)
-        finish(1)
-        finish(2)
+        for b in range(1, BLOCKS):
+            mix(b)
+            finish(b - 1)
+        finish(BLOCKS - 1)

@@ -25,8 +25,8 @@ LINE = 4
 LIST_ROWS = 16
 SPARE = 16
 BLOCKS = S // P
-X_SCALAR = 352
-W1_SCALAR = (104, 64)
+X_SCALAR = 416
+X_PARTS = (1, 2)
 
 
 def tile_picked_mixup_none_e_kernel(tc, xT, w1, w2, lam, mu, offs, pos1, out):
@@ -45,13 +45,13 @@ def tile_picked_mixup_none_e_kernel(tc, xT, w1, w2, lam, mu, offs, pos1, out):
             nc.vector.quantize_mx(out=codes[:].bitcast(FP8X4), scales=scales[:], in_=values)
             return codes, scales
 
-        def product(acc, left, cols, right, start, stop):
+        def product(acc, left, cols, right, start, stop, rcols=slice(None)):
             nc.tensor.matmul_mx(
                 out=acc,
                 lhsT=left[0][:, cols].bitcast(FP8X4),
                 lhsT_scale=left[1][:, cols],
-                rhs=right[0][:].bitcast(FP8X4),
-                rhs_scale=right[1][:],
+                rhs=right[0][:, rcols].bitcast(FP8X4),
+                rhs_scale=right[1][:, rcols],
                 start=start,
                 stop=stop,
             )
@@ -83,9 +83,13 @@ def tile_picked_mixup_none_e_kernel(tc, xT, w1, w2, lam, mu, offs, pos1, out):
         for t in range(PACK):
             nc.gpsimd.memset(h_sb[t][:, S:], 0.0)
 
-        picked = [tile("picked%d" % g, [P, 2, 2 * S], BF16) for g in range(PASSES)]
+        picked = [
+            [tile("picked%d_%d" % (g, n), [P, 2, 2 * S // X_PARTS[g]], BF16) for n in range(X_PARTS[g])]
+            for g in range(PASSES)
+        ]
 
         def pick(i):
+            g, u = divmod(i, 2)
             pairs = tile("pairs%d" % i, [P, T, 2], BF16)
             for copy, cols in ((nc.scalar.copy, slice(0, X_SCALAR)), (nc.vector.tensor_copy, slice(X_SCALAR, T))):
                 copy(
@@ -93,50 +97,78 @@ def tile_picked_mixup_none_e_kernel(tc, xT, w1, w2, lam, mu, offs, pos1, out):
                     in_=x_raw[i][:, :, cols].rearrange("p e (c i) -> p c e i", i=LINE),
                 )
             window = pairs[:].rearrange("p t e -> p (t e)").bitcast(U32)
-            nc.vector.tensor_copy(out=picked[i // 2][:, i % 2, :].bitcast(U32), in_=window.indirect(offs_sb[:]))
+            step = S // LIST_ROWS // X_PARTS[g]
+            for n in range(X_PARTS[g]):
+                places = offs_sb[:, n * step : (n + 1) * step]
+                nc.vector.tensor_copy(out=picked[g][n][:, u, :].bitcast(U32), in_=window.indirect(places))
 
         def weave(g, copy, word, tag):
-            woven = tile("woven%d" % g, [P, S * PACK], BF16, tag=tag)
-            words = picked[g][:].rearrange("p u n -> p (u n)").bitcast(word)
-            copy(
-                out=woven[:].bitcast(word).rearrange("p (c i u) -> p c u i", i=LINE, u=2),
-                in_=words.rearrange("p (u c i) -> p c u i", u=2, i=LINE),
-            )
-            return quantize("x%d" % g, woven[:], S)
-
-        for i in range(2 * PASSES):
-            pick(i)
-        xq = [weave(0, nc.scalar.copy, U32, "x_raw3"), weave(1, nc.vector.tensor_copy, I32, None)]
-
-        grouped = [tile("w1_grouped%d" % g, [P, PACK, P, PACK], BF16) for g in range(PASSES)]
-
-        def group(g):
-            cut = W1_SCALAR[g]
-            for copy, ms in ((nc.scalar.copy, slice(0, cut)), (nc.vector.tensor_copy, slice(cut, P))):
+            woven = []
+            for n in range(X_PARTS[g]):
+                woven.append(tile("woven%d_%d" % (g, n), [P, S // X_PARTS[g] * PACK], BF16, tag=tag))
+                words = picked[g][n][:].rearrange("p u n -> p (u n)").bitcast(word)
                 copy(
-                    out=grouped[g][:, :, ms, :].rearrange("p t m j -> p m j t"),
-                    in_=w1_raw[g][:].rearrange("p j (m t) -> p m j t", t=PACK)[:, ms],
+                    out=woven[n][:].bitcast(word).rearrange("p (c i u) -> p c u i", i=LINE, u=2),
+                    in_=words.rearrange("p (u c i) -> p c u i", u=2, i=LINE),
                 )
+            return woven
+
+        def quantize_x(g, woven, tag):
+            width = S // X_PARTS[g]
+            codes = tile("x%d_codes" % g, [P, S], U32, tag=tag)
+            scales = tile("x%d_scales" % g, [P, S], U8)
+            for n in range(X_PARTS[g]):
+                cols = slice(n * width, (n + 1) * width)
+                nc.vector.quantize_mx(out=codes[:, cols].bitcast(FP8X4), scales=scales[:, cols], in_=woven[n][:])
+            return codes, scales
+
+        for i in range(3):
+            pick(i)
+        woven = weave(0, nc.scalar.copy, U32, "x_raw2")
+        pick(3)
+        xq = [quantize_x(0, woven, "x_raw3")]
+        xq.append(quantize_x(1, weave(1, nc.vector.tensor_copy, I32, None), None))
+
+        grouped = [[tile("w1_grouped%d_%d" % (g, n), [P, 2, P, PACK], BF16) for n in range(2)] for g in range(PASSES)]
+
+        def group(g, first, copy):
+            ts = slice(first, first + 2)
+            copy(
+                out=grouped[g][first // 2][:].rearrange("p t m j -> p m j t"),
+                in_=w1_raw[g][:].rearrange("p j (m t) -> p m j t", t=PACK)[:, :, :, ts],
+            )
 
         w1q = {}
 
         def quantize_w1(g, first, count, tag=None):
-            values = grouped[g][:, first : first + count].rearrange("p t m j -> p (t m j)")
+            values = grouped[g][first // 2][:, first % 2 : first % 2 + count].rearrange("p t m j -> p (t m j)")
             planes = quantize("w1_%d_%d" % (g, first), values, count * P, tag=tag)
             for n in range(count):
                 w1q[g, first + n] = (planes, slice(n * P, (n + 1) * P))
 
-        group(0)
+        group(0, 0, nc.scalar.copy)
+        group(0, 2, nc.scalar.copy)
         quantize_w1(0, 0, 2)
-        group(1)
+        group(1, 0, nc.vector.tensor_copy)
+        group(1, 2, nc.scalar.copy)
         quantize_w1(1, 0, 1)
         quantize_w1(1, 1, 1)
         quantize_w1(0, 2, 2, tag="w1_raw1")
         quantize_w1(1, 2, 2)
-        h_ps = [psum.tile([P, S], F32, name="h_ps%d" % t, tag="bank_a%d" % t) for t in range(PACK)]
+        h_parts = []
         for t in range(PACK):
-            for g in range(PASSES):
-                product(h_ps[t][:], w1q[g, t][0], w1q[g, t][1], xq[g], g == 0, g == PASSES - 1)
+            pieces = [("bank_a%d" % t, slice(0, S), nc.scalar.copy)]
+            if t == 0:
+                pieces = [
+                    ("bank_a0", slice(0, S // 2), nc.scalar.copy),
+                    ("bank_b3", slice(S // 2, S), nc.vector.tensor_copy),
+                ]
+            h_parts.append([])
+            for n, (bank, cols, copy) in enumerate(pieces):
+                acc = psum.tile([P, cols.stop - cols.start], F32, name="h_ps%d_%d" % (t, n), tag=bank)
+                for g in range(PASSES):
+                    product(acc[:], w1q[g, t][0], w1q[g, t][1], xq[g], g == 0, g == PASSES - 1, cols)
+                h_parts[t].append((acc, cols, copy))
 
         w2_grouped = tile("w2_grouped", [P, N, PACK], BF16)
         nc.scalar.copy(
@@ -146,9 +178,13 @@ def tile_picked_mixup_none_e_kernel(tc, xT, w1, w2, lam, mu, offs, pos1, out):
         w2q = quantize("w2", w2_grouped[:].rearrange("p n j -> p (n j)"), N)
 
         partner = tile("partner", [P, PACK, S], F32)
-        turned_ps = [psum.tile([P, PACK, P], F32, name="turned_ps%d" % b, tag="bank_b%d" % b) for b in range(BLOCKS)]
+        turned_ps = []
         for t in range(PACK):
-            nc.scalar.copy(out=h_sb[t][:, :S], in_=h_ps[t][:])
+            for acc, cols, copy in h_parts[t]:
+                copy(out=h_sb[t][:, cols], in_=acc[:])
+            if t == 0:
+                for b in range(BLOCKS):
+                    turned_ps.append(psum.tile([P, PACK, P], F32, name="turned_ps%d" % b, tag="bank_b%d" % b))
             nc.vector.tensor_tensor(partner[:, t, :], h_sb[t][:].indirect(pos_sb[:]), mu_sb[:], MULT)
             for b in range(BLOCKS):
                 nc.tensor.transpose(turned_ps[b][:, t, :], h_sb[t][:, b * P : (b + 1) * P], ident[:])

from contextlib import ExitStack

import concourse.mybir as mybir
from concourse.masks import make_identity

K, T, S, H, N = 1024, 1024, 512, 512, 256
FLOPS = 2 * K * H * S + 2 * H * N * S

F32 = mybir.dt.float32
BF16 = mybir.dt.bfloat16
I32 = mybir.dt.int32
U32 = mybir.dt.uint32
U16 = mybir.dt.uint16
U8 = mybir.dt.uint8
FP8X4 = mybir.dt.float8_e4m3fn_x4
MULT = mybir.AluOpType.mult
ADD = mybir.AluOpType.add
COPY = mybir.ActivationFunctionType.Copy

P = 128
PACK = 4
K_PASS = P * PACK
PASSES = K // K_PASS
LINE = 4
LIST_ROWS = 16
SPARE = 16
BLOCKS = S // P
X_SCALAR = 416
X_PARTS = (1, 2)


def tile_picked_mixup_none_e_kernel(tc, xT, w1, w2, lam, mu, offs, pos1, out):
    nc = tc.nc

    with ExitStack() as ctx:
        sb = ctx.enter_context(tc.tile_pool(name="sb", bufs=1))
        psum = ctx.enter_context(tc.psum_pool(name="psum", bufs=1))

        def tile(name, shape, dtype, tag=None):
            return sb.tile(shape, dtype, name=name, tag=tag or name, align_bytes=64)

        def quantize(name, values, width, tag=None):
            codes = tile(name + "_codes", [P, width], U32, tag=tag)
            scales = tile(name + "_scales", [P, width], U8)
            nc.vector.quantize_mx(out=codes[:].bitcast(FP8X4), scales=scales[:], in_=values)
            return codes, scales

        def product(acc, left, cols, right, start, stop, rcols=slice(None)):
            nc.tensor.matmul_mx(
                out=acc,
                lhsT=left[0][:, cols].bitcast(FP8X4),
                lhsT_scale=left[1][:, cols],
                rhs=right[0][:, rcols].bitcast(FP8X4),
                rhs_scale=right[1][:, rcols],
                start=start,
                stop=stop,
            )

        offs_sb = sb.tile([P, S // LIST_ROWS], U16, name="offs_sb")
        pos_sb = sb.tile([P, S // LIST_ROWS], U16, name="pos_sb")
        x_raw = [tile("x_raw%d" % i, [P, 2, T], F32) for i in range(2 * PASSES)]
        w1_raw = [tile("w1_raw%d" % g, [P, PACK, H], F32) for g in range(PASSES)]
        w2_raw = tile("w2_raw", [P, PACK, N], F32)
        mu_sb = tile("mu_sb", [P, S], F32)
        lam_col = tile("lam_col", [P, BLOCKS], F32)
        x_view = xT.rearrange("(g p u e) t -> g u p e t", p=P, u=2, e=2)
        for i in range(2 * PASSES):
            nc.sync.dma_start(out=x_raw[i][:], in_=x_view[i // 2, i % 2])
            if i == 0:
                nc.sync.dma_start(offs_sb[:], offs)
        w1_view = w1.rearrange("(g p j) c -> g p j c", p=P, j=PACK)
        for g in range(PASSES):
            nc.sync.dma_start(out=w1_raw[g][:], in_=w1_view[g])
        nc.sync.dma_start(out=w2_raw[:], in_=w2.rearrange("(p j) c -> p j c", j=PACK))
        nc.sync.dma_start(pos_sb[:], pos1)
        nc.sync.dma_start(out=mu_sb[:], in_=mu)
        with nc.allow_non_contiguous_dma(reason="one share a partition"):
            nc.sync.dma_start(out=lam_col[:], in_=lam[0:1, :].rearrange("o (b p) -> p (o b)", p=P))

        ident = tile("ident", [P, P], F32)
        make_identity(nc, ident[:])
        h_sb = [tile("h_sb%d" % t, [P, S + SPARE], F32) for t in range(PACK)]
        for t in range(PACK):
            nc.gpsimd.memset(h_sb[t][:, S:], 0.0)

        picked = [
            [tile("picked%d_%d" % (g, n), [P, 2, 2 * S // X_PARTS[g]], BF16) for n in range(X_PARTS[g])]
            for g in range(PASSES)
        ]

        def pick(i):
            g, u = divmod(i, 2)
            pairs = tile("pairs%d" % i, [P, T, 2], BF16)
            for copy, cols in ((nc.scalar.copy, slice(0, X_SCALAR)), (nc.vector.tensor_copy, slice(X_SCALAR, T))):
                copy(
                    out=pairs[:, cols, :].rearrange("p (c i) e -> p c e i", i=LINE),
                    in_=x_raw[i][:, :, cols].rearrange("p e (c i) -> p c e i", i=LINE),
                )
            window = pairs[:].rearrange("p t e -> p (t e)").bitcast(U32)
            step = S // LIST_ROWS // X_PARTS[g]
            for n in range(X_PARTS[g]):
                places = offs_sb[:, n * step : (n + 1) * step]
                nc.vector.tensor_copy(out=picked[g][n][:, u, :].bitcast(U32), in_=window.indirect(places))

        def weave(g, copy, word, tag):
            woven = []
            for n in range(X_PARTS[g]):
                woven.append(tile("woven%d_%d" % (g, n), [P, S // X_PARTS[g] * PACK], BF16, tag=tag))
                words = picked[g][n][:].rearrange("p u n -> p (u n)").bitcast(word)
                copy(
                    out=woven[n][:].bitcast(word).rearrange("p (c i u) -> p c u i", i=LINE, u=2),
                    in_=words.rearrange("p (u c i) -> p c u i", u=2, i=LINE),
                )
            return woven

        def quantize_x(g, woven, tag):
            width = S // X_PARTS[g]
            codes = tile("x%d_codes" % g, [P, S], U32, tag=tag)
            scales = tile("x%d_scales" % g, [P, S], U8)
            for n in range(X_PARTS[g]):
                cols = slice(n * width, (n + 1) * width)
                nc.vector.quantize_mx(out=codes[:, cols].bitcast(FP8X4), scales=scales[:, cols], in_=woven[n][:])
            return codes, scales

        for i in range(3):
            pick(i)
        woven = weave(0, nc.scalar.copy, U32, "x_raw2")
        pick(3)
        xq = [quantize_x(0, woven, "x_raw3")]
        xq.append(quantize_x(1, weave(1, nc.vector.tensor_copy, I32, None), None))

        grouped = [[tile("w1_grouped%d_%d" % (g, n), [P, 2, P, PACK], BF16) for n in range(2)] for g in range(PASSES)]

        def group(g, first, copy):
            ts = slice(first, first + 2)
            copy(
                out=grouped[g][first // 2][:].rearrange("p t m j -> p m j t"),
                in_=w1_raw[g][:].rearrange("p j (m t) -> p m j t", t=PACK)[:, :, :, ts],
            )

        w1q = {}

        def quantize_w1(g, first, count, tag=None):
            values = grouped[g][first // 2][:, first % 2 : first % 2 + count].rearrange("p t m j -> p (t m j)")
            planes = quantize("w1_%d_%d" % (g, first), values, count * P, tag=tag)
            for n in range(count):
                w1q[g, first + n] = (planes, slice(n * P, (n + 1) * P))

        group(0, 0, nc.scalar.copy)
        group(0, 2, nc.scalar.copy)
        quantize_w1(0, 0, 2)
        group(1, 0, nc.vector.tensor_copy)
        group(1, 2, nc.scalar.copy)
        quantize_w1(1, 0, 1)
        quantize_w1(1, 1, 1)
        quantize_w1(0, 2, 2, tag="w1_raw1")
        quantize_w1(1, 2, 2)
        h_parts = []
        for t in range(PACK):
            pieces = [("bank_a%d" % t, slice(0, S), nc.scalar.copy)]
            if t == 0:
                pieces = [
                    ("bank_a0", slice(0, S // 2), nc.scalar.copy),
                    ("bank_b3", slice(S // 2, S), nc.vector.tensor_copy),
                ]
            h_parts.append([])
            for n, (bank, cols, copy) in enumerate(pieces):
                acc = psum.tile([P, cols.stop - cols.start], F32, name="h_ps%d_%d" % (t, n), tag=bank)
                for g in range(PASSES):
                    product(acc[:], w1q[g, t][0], w1q[g, t][1], xq[g], g == 0, g == PASSES - 1, cols)
                h_parts[t].append((acc, cols, copy))

        w2_grouped = tile("w2_grouped", [P, N, PACK], BF16)
        nc.scalar.copy(
            out=w2_grouped[:].rearrange("p (c i) j -> p c j i", i=LINE),
            in_=w2_raw[:].rearrange("p j (c i) -> p c j i", i=LINE),
        )
        w2q = quantize("w2", w2_grouped[:].rearrange("p n j -> p (n j)"), N)

        partner = tile("partner", [P, PACK, S], F32)
        turned_ps = []
        for t in range(PACK):
            for acc, cols, copy in h_parts[t]:
                copy(out=h_sb[t][:, cols], in_=acc[:])
            if t == 0:
                for b in range(BLOCKS):
                    turned_ps.append(psum.tile([P, PACK, P], F32, name="turned_ps%d" % b, tag="bank_b%d" % b))
            nc.vector.tensor_tensor(partner[:, t, :], h_sb[t][:].indirect(pos_sb[:]), mu_sb[:], MULT)
            for b in range(BLOCKS):
                nc.tensor.transpose(turned_ps[b][:, t, :], h_sb[t][:, b * P : (b + 1) * P], ident[:])

        own_ps = []
        for b in range(BLOCKS):
            turned = tile("turned%d" % b, [P, PACK, P], F32)
            nc.scalar.activation(turned[:], turned_ps[b][:], COPY, scale=lam_col[:, b : b + 1])
            own_ps.append(psum.tile([P, PACK, P], F32, name="own_ps%d" % b, tag="bank_a%d" % b))
            for t in range(PACK):
                nc.tensor.transpose(own_ps[b][:, t, :], turned[:, t, :], ident[:])

        z_bf = [tile("z_bf%d" % b, [P, P, PACK], BF16) for b in range(BLOCKS)]
        out_view = out.rearrange("(r p) s -> p r s", p=P)

        def mix(b):
            nc.vector.tensor_tensor(
                z_bf[b][:].rearrange("p (c i) t -> p c t i", i=LINE),
                own_ps[b][:].rearrange("p t (c i) -> p c t i", i=LINE),
                partner[:, :, b * P : (b + 1) * P].rearrange("p t (c i) -> p c t i", i=LINE),
                ADD,
            )

        def finish(b):
            zq = quantize("z%d" % b, z_bf[b][:].rearrange("p n t -> p (n t)"), P)
            o_ps = psum.tile([P, N // P, P], F32, name="o_ps%d" % b, tag="bank_b%d" % b)
            for r in range(N // P):
                product(o_ps[:, r, :], w2q, slice(r * P, (r + 1) * P), zq, True, True)
            o_sb = tile("o_sb%d" % b, [P, N // P, P], F32)
            nc.scalar.copy(out=o_sb[:], in_=o_ps[:])
            nc.sync.dma_start(out=out_view[:, :, b * P : (b + 1) * P], in_=o_sb[:])

        mix(0)
        for b in range(1, BLOCKS):
            mix(b)
            finish(b - 1)
        finish(BLOCKS - 1)
